import numpy as np
import ml_dtypes


def mxq(x, axis, fmt="e4m3"):
    dtype, down = {"e4m3": (ml_dtypes.float8_e4m3fn, 7), "e5m2": (ml_dtypes.float8_e5m2, 14)}[fmt]
    v = np.moveaxis(np.asarray(x, np.float32).astype(ml_dtypes.bfloat16).astype(np.float64), axis, -1)
    blocks = v.reshape(v.shape[:-1] + (-1, 32))
    amax = np.abs(blocks).max(-1, keepdims=True)
    byte = np.maximum(np.where(amax > 0, np.frexp(amax)[1] - 1 + 127, 0) - down, 1)
    scale = np.exp2(byte - 127.0)
    codes = (blocks / scale).astype(np.float32).astype(dtype).astype(np.float64)
    return np.moveaxis((codes * scale).reshape(v.shape), -1, axis)


WIDE = False


def mx_kscale(k):
    if not WIDE:
        return np.ones(k)
    levels = np.array([10, -10, 5, -5, 0])
    if k % 512:
        return np.exp2(np.random.permutation(np.resize(levels, k // 32))).repeat(32)
    a = np.empty((k // 512, 16))
    for p in range(k // 512):
        a[p, :8] = np.random.permutation(np.resize(levels, 8))
        for g in range(8):
            far = levels[np.abs(levels - a[p, g]) >= 10]
            a[p, g + 8] = far[np.random.randint(len(far))]
    return np.exp2(a.ravel()).repeat(32)


def f64(x):
    return np.asarray(x).astype(np.float64)


def striped(idx):
    return np.tile(np.asarray(idx).reshape(-1, 16).T, (8, 1)).astype(np.uint16)


def unstriped(offs):
    return offs[:16].T.reshape(-1).astype(np.int64)


E2M1 = np.array([0.0, 0.5, 1.0, 1.5, 2.0, 3.0, 4.0, 6.0, -0.0, -0.5, -1.0, -1.5, -2.0, -3.0, -4.0, -6.0])


def pack_weight(w, fmt):
    k, n = w.shape
    w = f64(np.asarray(w, np.float32).astype(ml_dtypes.bfloat16)).reshape(k // 32, 32, n)
    amax = np.abs(w).max(1)
    if fmt == "e4m3":
        byte = np.frexp(amax)[1] - 1 + 127 - 7
    else:
        mant, ex = np.frexp(amax / 6.0)
        byte = np.where(mant > 0.5, ex, ex - 1) + 127
    byte = np.clip(np.where(amax > 0, byte, 1), 1, 254)
    scaled = (w * np.exp2(127.0 - byte)[:, None, :]).reshape(k, n).astype(np.float32)
    by_word = np.ascontiguousarray(scaled.reshape(k // 512, 128, 4, n).transpose(0, 1, 3, 2))
    if fmt == "e4m3":
        words = by_word.astype(ml_dtypes.float8_e4m3fn).view(np.uint8)
    else:
        c = by_word.astype(ml_dtypes.float4_e2m1fn).view(np.uint8) & 0xF
        words = (c[..., 0::2] | (c[..., 1::2] << 4)).reshape(k // 512, 128, 2 * n)
    return np.ascontiguousarray(words), np.ascontiguousarray(byte.astype(np.uint8).reshape(k // 512, 16, n))


def unpack_weight(words, scales, fmt):
    g, _, n = scales.shape
    words = np.ascontiguousarray(words).reshape(g, 128, n, -1)
    if fmt == "e4m3":
        vals = words.view(ml_dtypes.float8_e4m3fn).astype(np.float64)
    else:
        nib = np.empty((g, 128, n, 4), np.uint8)
        nib[..., 0::2] = words & 0xF
        nib[..., 1::2] = words >> 4
        vals = E2M1[nib]
    vals = vals * np.repeat(np.exp2(scales.astype(np.float64) - 127.0), 8, axis=1)[..., None]
    return vals.transpose(0, 1, 3, 2).reshape(g * 512, n)


D, T, I, Q, E, Z, X = 512, 2048, 512, 128, 512, 1024, 1024


def setup_inputs():
    n = np.random.standard_normal
    idx = np.random.permutation(T)[:I]
    idx2 = np.random.permutation(Z)[:I]
    idx3 = np.random.permutation(Z)[:I]
    idx4 = np.random.permutation(X)[:I]
    fd = mx_kscale(D)
    fi = mx_kscale(I)
    ti = np.ones(T)
    ti[idx] = fi
    ti4 = np.ones(X)
    ti4[idx4] = fi
    keysp = pack_weight(n((D, T)) / fd[:, None], "e4m3")
    return {
        "query": (n((D, Q)) * 1.0 / np.sqrt(D) * fd[:, None]).astype(np.float32),
        "keys_words": keysp[0],
        "keys_scales": keysp[1],
        "os": (np.random.uniform(0.02, 0.08, (1, I)) * fi).astype(np.float32),
        "os2": (np.random.uniform(0.02, 0.08, (1, I)) * fi).astype(np.float32),
        "vals": (n((E, T)) / ti).astype(np.float32),
        "vals2": (n((E, X)) / ti4).astype(np.float32),
        "offs": striped(idx),
        "offs2": striped(idx2),
        "offs3": striped(idx3),
        "offs4": striped(idx4),
    }


def reference(query, keys_words, keys_scales, os, os2, vals, vals2, offs, offs2, offs3, offs4):
    idx = unstriped(offs)
    idx2 = unstriped(offs2)
    idx3 = unstriped(offs3)
    idx4 = unstriped(offs4)
    keysu = unpack_weight(keys_words, keys_scales, "e4m3")
    queryq = mxq(f64(query), 0, "e4m3")
    keysidxg = keysu[:, idx]
    a = queryq.T @ keysidxg
    f0 = np.zeros((Q, Z))
    f0[:, idx2] = a
    s = a + f0[:, idx3]
    w = np.maximum(s, 0.0)
    wo1 = w * f64(os)
    wt1 = wo1.T
    wo2 = w * f64(os2)
    wt2 = wo2.T
    vt1 = f64(vals)[:, idx].T
    vt2 = f64(vals2)[:, idx4].T
    wt1q = mxq(wt1, 0, "e4m3")
    vt1q = mxq(vt1, 0, "e4m3")
    wt2q = mxq(wt2, 0, "e4m3")
    vt2q = mxq(vt2, 0, "e4m3")
    o = wt1q.T @ vt1q + wt2q.T @ vt2q
    return o

@@ -1,0 +1,204 @@
+from contextlib import ExitStack
+
+import concourse.mybir as mybir
+from concourse.masks import make_identity
+
+F32 = mybir.dt.float32
+BF16 = mybir.dt.bfloat16
+I32 = mybir.dt.int32
+U32 = mybir.dt.uint32
+U16 = mybir.dt.uint16
+U8 = mybir.dt.uint8
+FP8X4 = mybir.dt.float8_e4m3fn_x4
+ALU = mybir.AluOpType
+COPY = mybir.ActivationFunctionType.Copy
+
+D, T, I, Q, E, Z, X = 512, 2048, 512, 128, 512, 1024, 1024
+P = 128
+FLOPS = 2 * Q * I * D + 2 * 2 * Q * I * E
+HALF = I // 2
+NB = E // P
+W = 4 * P
+LAST_SPLIT = 20
+
+
+def tile_attend_passedthrough_twostores_lean_kernel(
+    tc, query, keys_words, keys_scales, factor1, factor2, vals, vals2, offs, offs2, offs3, offs4, out
+):
+    nc = tc.nc
+    with ExitStack() as ctx:
+        sb = ctx.enter_context(tc.tile_pool(name="sb", bufs=1))
+        ps = ctx.enter_context(tc.psum_pool(name="ps", bufs=1))
+
+        def tile(shape, dtype, name, on=None):
+            return sb.tile(shape, dtype, name=name, tag=on or name, align_bytes=64)
+
+        def bank(shape, name, on=None):
+            return ps.tile(shape, F32, name=name, tag=on or name)
+
+        l1 = tile([P, I // 16], U16, "l1")
+        l2 = tile([P, I // 16], U16, "l2")
+        l3 = tile([P, I // 16], U16, "l3")
+        l4 = tile([P, I // 16], U16, "l4")
+        kw = tile([P, T], U32, "kw")
+        ks = tile([P, T], U8, "ks")
+        q_raw = tile([P, 4, Q], F32, "q_raw")
+        f0 = tile([P, Z], F32, "f0")
+        fac = [tile([P, 4], F32, "fac%d" % s) for s in range(2)]
+        pool1 = [tile([P, T], F32, "pool1_%d" % j) for j in range(NB)]
+        pool2 = [tile([P, X], F32, "pool2_%d" % j) for j in range(NB)]
+        ident = tile([P, P], F32, "ident")
+
+        nc.vector.memset(ks[:].bitcast(I32), 0)
+        nc.vector.memset(f0[:], 0.0)
+        make_identity(nc, ident[:])
+
+        def load1(j):
+            nc.sync.dma_start(pool1[j][:], vals[j * P : (j + 1) * P, :])
+
+        def load2(j):
+            nc.sync.dma_start(pool2[j][:], vals2[j * P : (j + 1) * P, :])
+
+        nc.sync.dma_start(l1[:], offs)
+        nc.sync.dma_start(q_raw[:], query.rearrange("(p j) w -> p j w", j=4))
+        nc.sync.dma_start(kw[:].bitcast(I32), keys_words[0].rearrange("p n t -> p (n t)").bitcast(I32))
+        for g in range(4):
+            nc.sync.dma_start(
+                ks[32 * g : 32 * g + 4, :].bitcast(I32), keys_scales[0, 4 * g : 4 * g + 4, :].bitcast(I32)
+            )
+        nc.sync.dma_start(l4[:], offs4)
+        load2(0)
+        load2(1)
+        nc.sync.dma_start(l2[:], offs2)
+        load2(2)
+        nc.sync.dma_start(l3[:], offs3)
+        load2(3)
+        for s, factor in enumerate((factor1, factor2)):
+            nc.sync.dma_start(fac[s][:], factor.rearrange("o (p t) -> (o p) t", t=4))
+        for j in range(NB):
+            load1(j)
+
+        def gather(engine, dst, window, lst):
+            if engine == "V":
+                nc.vector.tensor_copy(dst, window.indirect(lst))
+            else:
+                nc.scalar.activation(dst, window.indirect(lst), COPY)
+
+        def turn(s, j, engine, turned):
+            window, lst = (pool1[j], l1) if s == 0 else (pool2[j], l4)
+            g = tile([P, I], BF16, "g%d_%d" % (s, j))
+            if engine == "both":
+                n = LAST_SPLIT * 16
+                gather("V", g[:, :n], window[:], lst[:, :LAST_SPLIT])
+                gather("S", g[:, n:], window[:], lst[:, LAST_SPLIT:])
+            else:
+                gather(engine, g[:], window[:], lst[:])
+            words = g[:].bitcast(F32)
+            for u in range(2):
+                nc.tensor.transpose(turned[:, u, :], words[:, u::2], ident[:])
+
+        def weave(engine, dst_words, turned):
+            dst = dst_words.rearrange("p (b e u) -> p b e u", u=2, e=P)
+            src = turned.rearrange("p b u e -> p b e u")
+            if engine == "V":
+                nc.vector.tensor_copy(dst, src)
+            else:
+                nc.scalar.copy(dst, src)
+
+        def quantise(src, name, on=None):
+            n = src.shape[1] // 4
+            c = tile([P, n], U32, name + "_codes", on)
+            sc = tile([P, n], U8, name + "_scales")
+            nc.vector.quantize_mx(out=c[:].bitcast(FP8X4), scales=sc[:], in_=src)
+            return c, sc
+
+        def product(dst, lhs, lcols, rhs, rcols, start, stop):
+            nc.tensor.matmul_mx(
+                out=dst, lhsT=lhs[0][:, lcols].bitcast(FP8X4), lhsT_scale=lhs[1][:, lcols],
+                rhs=rhs[0][:, rcols].bitcast(FP8X4), rhs_scale=rhs[1][:, rcols], start=start, stop=stop,
+            )
+
+        q_bf = tile([P, Q, 4], BF16, "q_bf")
+        nc.scalar.activation(q_bf[:], q_raw[:].rearrange("p j w -> p w j"), COPY)
+        q_mx = quantise(q_bf[:].rearrange("p w j -> p (w j)"), "q")
+
+        t_ab = bank([P, 2, 2, P], "t_ab")
+        turn(1, 0, "S", t_ab[:, 0])
+
+        a_sb = tile([P, I], F32, "a_sb", on="pool2_0")
+        for h in range(2):
+            kg = tile([P, HALF], U32, "kg%d" % h)
+            sg = tile([P, HALF], U8, "sg%d" % h)
+            cols = slice(h * 16, (h + 1) * 16)
+            nc.vector.tensor_copy(kg[:], kw[:].indirect(l1[:, cols]))
+            nc.vector.tensor_copy(sg[:], ks[:].indirect(l1[:, cols]))
+            a_ps = bank([P, HALF], "a_ps%d" % h)
+            product(a_ps[:], q_mx, slice(0, Q), (kg, sg), slice(0, HALF), True, True)
+            slots = slice(h * HALF, (h + 1) * HALF)
+            nc.scalar.copy(a_sb[:, slots], a_ps[:])
+            nc.scalar.activation(f0[:].indirect(l2[:, cols]), a_sb[:, slots], COPY)
+
+        s_ps = bank([P, 4, Q], "s_ps")
+        for t in range(4):
+            nc.tensor.matmul(s_ps[:, t, :], a_sb[:, t::4], ident[:], start=(t == 0), stop=False, is_transpose=True)
+
+        turn(1, 1, "V", t_ab[:, 1])
+        t_cd = bank([P, 2, 2, P], "t_cd")
+        turn(1, 2, "V", t_cd[:, 0])
+        turn(1, 3, "V", t_cd[:, 1])
+        v2_bf = tile([P, NB * W], BF16, "v2_bf", on="pool2_0")
+        weave("S", v2_bf[:, : 2 * W].bitcast(F32), t_ab[:])
+        weave("S", v2_bf[:, 2 * W :].bitcast(F32), t_cd[:])
+
+        t_ef = bank([P, 2, 2, P], "t_ef")
+        turn(0, 0, "V", t_ef[:, 0])
+
+        looked = tile([P, I], F32, "looked", on="pool1_0")
+        nc.vector.tensor_copy(looked[:], f0[:].indirect(l3[:]))
+        for t in range(4):
+            nc.tensor.matmul(s_ps[:, t, :], looked[:, t::4], ident[:], start=False, stop=(t == 3), is_transpose=True)
+        v2_mx = quantise(v2_bf[:], "v2", on="f0")
+
+        w_bf = tile([P, 2, Q, 4], BF16, "w_bf")
+        for s in range(2):
+            nc.vector.scalar_tensor_tensor(
+                w_bf[:, s], s_ps[:].rearrange("p t q -> p q t"), 0.0,
+                fac[s][:].unsqueeze(1).to_broadcast([P, Q, 4]), ALU.max, ALU.mult,
+            )
+        turn(0, 1, "S", t_ef[:, 1])
+        w_mx = quantise(w_bf[:].rearrange("p s q t -> p (s q t)"), "w")
+        w1, w2 = slice(0, Q), slice(Q, 2 * Q)
+
+        o01 = bank([P, 2 * P], "o01", on="a_ps0")
+        o2 = bank([P, P], "o2", on="a_ps1")
+        o3 = bank([P, P], "o3")
+        product(o01[:], w_mx, w2, v2_mx, slice(0, 2 * P), True, False)
+        product(o2[:], w_mx, w2, v2_mx, slice(2 * P, 3 * P), True, False)
+        product(o3[:], w_mx, w2, v2_mx, slice(3 * P, 4 * P), True, False)
+
+        t_g = bank([P, 1, 2, P], "t_g", on="t_ab")
+        turn(0, 2, "S", t_g[:, 0])
+
+        ef_bf = tile([P, 2 * W], BF16, "ef_bf")
+        weave("V", ef_bf[:].bitcast(F32), t_ef[:])
+        ef_mx = quantise(ef_bf[:], "ef")
+        product(o01[:], w_mx, w1, ef_mx, slice(0, 2 * P), False, True)
+
+        t_h = bank([P, 1, 2, P], "t_h", on="t_cd")
+        turn(0, 3, "both", t_h[:, 0])
+
+        late = tile([P, 7 * P], F32, "late", on="pool1_3")
+        g_words, h_words, res = late[:, : 2 * P], late[:, 2 * P : 4 * P], late[:, 4 * P :]
+        weave("S", g_words, t_g[:])
+        nc.scalar.copy(res[:, : 2 * P], o01[:])
+        nc.sync.dma_start(out[:, : 2 * P], res[:, : 2 * P])
+        g_mx = quantise(g_words.bitcast(BF16), "g")
+        product(o2[:], w_mx, w1, g_mx, slice(0, P), False, True)
+        weave("V", h_words, t_h[:])
+        h_mx = quantise(h_words.bitcast(BF16), "h")
+        product(o3[:], w_mx, w1, h_mx, slice(0, P), False, True)
+        nc.scalar.copy(res[:, 2 * P :], o2[:])
+        nc.sync.dma_start(out[:, 2 * P : 3 * P], res[:, 2 * P :])
+        res3 = tile([P, P], F32, "res3")
+        nc.vector.tensor_copy(res3[:], o3[:])
+        nc.sync.dma_start(out[:, 3 * P :], res3[:])

@@ -19,7 +19,7 @@ FLOPS = 2 * Q * I * D + 2 * 2 * Q * I * E
 HALF = I // 2
 NB = E // P
 W = 4 * P
-LAST_SPLIT = 20
+LAST_SPLIT = 18
 
 
 def tile_attend_passedthrough_twostores_lean_kernel(
@@ -52,6 +52,8 @@ def tile_attend_passedthrough_twostores_lean_kernel(
         nc.vector.memset(ks[:].bitcast(I32), 0)
         nc.vector.memset(f0[:], 0.0)
         make_identity(nc, ident[:])
+        for s, factor in enumerate((factor1, factor2)):
+            nc.gpsimd.dma_start(fac[s][:], factor.rearrange("o (p t) -> (o p) t", t=4))
 
         def load1(j):
             nc.sync.dma_start(pool1[j][:], vals[j * P : (j + 1) * P, :])
@@ -59,13 +61,12 @@ def tile_attend_passedthrough_twostores_lean_kernel(
         def load2(j):
             nc.sync.dma_start(pool2[j][:], vals2[j * P : (j + 1) * P, :])
 
-        nc.sync.dma_start(l1[:], offs)
         nc.sync.dma_start(q_raw[:], query.rearrange("(p j) w -> p j w", j=4))
+        nc.sync.dma_start(l1[:], offs)
         nc.sync.dma_start(kw[:].bitcast(I32), keys_words[0].rearrange("p n t -> p (n t)").bitcast(I32))
-        for g in range(4):
-            nc.sync.dma_start(
-                ks[32 * g : 32 * g + 4, :].bitcast(I32), keys_scales[0, 4 * g : 4 * g + 4, :].bitcast(I32)
-            )
+        scale_rows = keys_scales[0].rearrange("(g r) c -> r g c", r=4)
+        for r in range(4):
+            nc.sync.dma_start(ks[r:P:32, :].bitcast(I32), scale_rows[r].bitcast(I32))
         nc.sync.dma_start(l4[:], offs4)
         load2(0)
         load2(1)
@@ -73,8 +74,6 @@ def tile_attend_passedthrough_twostores_lean_kernel(
         load2(2)
         nc.sync.dma_start(l3[:], offs3)
         load2(3)
-        for s, factor in enumerate((factor1, factor2)):
-            nc.sync.dma_start(fac[s][:], factor.rearrange("o (p t) -> (o p) t", t=4))
         for j in range(NB):
             load1(j)
 
@@ -120,44 +119,47 @@ def tile_attend_passedthrough_twostores_lean_kernel(
 
         q_bf = tile([P, Q, 4], BF16, "q_bf")
         nc.scalar.activation(q_bf[:], q_raw[:].rearrange("p j w -> p w j"), COPY)
+
         q_mx = quantise(q_bf[:].rearrange("p w j -> p (w j)"), "q")
 
         t_ab = bank([P, 2, 2, P], "t_ab")
+        t_cd = bank([P, 2, 2, P], "t_cd")
         turn(1, 0, "S", t_ab[:, 0])
 
+        halves = [slice(h * 16, (h + 1) * 16) for h in range(2)]
+        kg = [tile([P, HALF], U32, "kg%d" % h) for h in range(2)]
+        for h in range(2):
+            nc.vector.tensor_copy(kg[h][:], kw[:].indirect(l1[:, halves[h]]))
         a_sb = tile([P, I], F32, "a_sb", on="pool2_0")
         for h in range(2):
-            kg = tile([P, HALF], U32, "kg%d" % h)
             sg = tile([P, HALF], U8, "sg%d" % h)
-            cols = slice(h * 16, (h + 1) * 16)
-            nc.vector.tensor_copy(kg[:], kw[:].indirect(l1[:, cols]))
-            nc.vector.tensor_copy(sg[:], ks[:].indirect(l1[:, cols]))
+            nc.vector.tensor_copy(sg[:], ks[:].indirect(l1[:, halves[h]]))
             a_ps = bank([P, HALF], "a_ps%d" % h)
-            product(a_ps[:], q_mx, slice(0, Q), (kg, sg), slice(0, HALF), True, True)
+            product(a_ps[:], q_mx, slice(0, Q), (kg[h], sg), slice(0, HALF), True, True)
             slots = slice(h * HALF, (h + 1) * HALF)
             nc.scalar.copy(a_sb[:, slots], a_ps[:])
-            nc.scalar.activation(f0[:].indirect(l2[:, cols]), a_sb[:, slots], COPY)
+            nc.scalar.activation(f0[:].indirect(l2[:, halves[h]]), a_sb[:, slots], COPY)
 
         s_ps = bank([P, 4, Q], "s_ps")
         for t in range(4):
             nc.tensor.matmul(s_ps[:, t, :], a_sb[:, t::4], ident[:], start=(t == 0), stop=False, is_transpose=True)
 
-        turn(1, 1, "V", t_ab[:, 1])
-        t_cd = bank([P, 2, 2, P], "t_cd")
-        turn(1, 2, "V", t_cd[:, 0])
-        turn(1, 3, "V", t_cd[:, 1])
-        v2_bf = tile([P, NB * W], BF16, "v2_bf", on="pool2_0")
-        weave("S", v2_bf[:, : 2 * W].bitcast(F32), t_ab[:])
-        weave("S", v2_bf[:, 2 * W :].bitcast(F32), t_cd[:])
+        for j in range(1, NB):
+            turn(1, j, "V", (t_ab, t_cd)[j // 2][:, j % 2])
+        ab_bf = tile([P, 2 * W], BF16, "ab_bf", on="pool2_2")
+        weave("V", ab_bf[:].bitcast(F32), t_ab[:])
 
-        t_ef = bank([P, 2, 2, P], "t_ef")
-        turn(0, 0, "V", t_ef[:, 0])
-
-        looked = tile([P, I], F32, "looked", on="pool1_0")
+        looked = tile([P, I], F32, "looked", on="pool2_3")
         nc.vector.tensor_copy(looked[:], f0[:].indirect(l3[:]))
         for t in range(4):
             nc.tensor.matmul(s_ps[:, t, :], looked[:, t::4], ident[:], start=False, stop=(t == 3), is_transpose=True)
-        v2_mx = quantise(v2_bf[:], "v2", on="f0")
+        ab_mx = quantise(ab_bf[:], "ab", on="f0")
+
+
+        t_ef = bank([P, 2, 2, P], "t_ef")
+        turn(0, 0, "S", t_ef[:, 0])
+        cd_bf = tile([P, 2 * W], BF16, "cd_bf", on="pool1_0")
+        weave("S", cd_bf[:].bitcast(F32), t_cd[:])
 
         w_bf = tile([P, 2, Q, 4], BF16, "w_bf")
         for s in range(2):
@@ -168,19 +170,15 @@ def tile_attend_passedthrough_twostores_lean_kernel(
         turn(0, 1, "S", t_ef[:, 1])
         w_mx = quantise(w_bf[:].rearrange("p s q t -> p (s q t)"), "w")
         w1, w2 = slice(0, Q), slice(Q, 2 * Q)
-
-        o01 = bank([P, 2 * P], "o01", on="a_ps0")
-        o2 = bank([P, P], "o2", on="a_ps1")
-        o3 = bank([P, P], "o3")
-        product(o01[:], w_mx, w2, v2_mx, slice(0, 2 * P), True, False)
-        product(o2[:], w_mx, w2, v2_mx, slice(2 * P, 3 * P), True, False)
-        product(o3[:], w_mx, w2, v2_mx, slice(3 * P, 4 * P), True, False)
+        cd_mx = quantise(cd_bf[:], "cd")
 
         t_g = bank([P, 1, 2, P], "t_g", on="t_ab")
         turn(0, 2, "S", t_g[:, 0])
 
         ef_bf = tile([P, 2 * W], BF16, "ef_bf")
         weave("V", ef_bf[:].bitcast(F32), t_ef[:])
+        o01 = bank([P, 2 * P], "o01", on="t_ef")
+        product(o01[:], w_mx, w2, ab_mx, slice(0, 2 * P), True, False)
         ef_mx = quantise(ef_bf[:], "ef")
         product(o01[:], w_mx, w1, ef_mx, slice(0, 2 * P), False, True)
 
@@ -189,12 +187,16 @@ def tile_attend_passedthrough_twostores_lean_kernel(
 
         late = tile([P, 7 * P], F32, "late", on="pool1_3")
         g_words, h_words, res = late[:, : 2 * P], late[:, 2 * P : 4 * P], late[:, 4 * P :]
-        weave("S", g_words, t_g[:])
+        weave("V", g_words, t_g[:])
         nc.scalar.copy(res[:, : 2 * P], o01[:])
         nc.sync.dma_start(out[:, : 2 * P], res[:, : 2 * P])
+        o2 = bank([P, P], "o2", on="t_ef")
+        product(o2[:], w_mx, w2, cd_mx, slice(0, P), True, False)
         g_mx = quantise(g_words.bitcast(BF16), "g")
         product(o2[:], w_mx, w1, g_mx, slice(0, P), False, True)
-        weave("V", h_words, t_h[:])
+        weave("S", h_words, t_h[:])
+        o3 = bank([P, P], "o3", on="t_cd")
+        product(o3[:], w_mx, w2, cd_mx, slice(P, 2 * P), True, False)
         h_mx = quantise(h_words.bitcast(BF16), "h")
         product(o3[:], w_mx, w1, h_mx, slice(0, P), False, True)
         nc.scalar.copy(res[:, 2 * P :], o2[:])

from contextlib import ExitStack

import concourse.mybir as mybir
from concourse.masks import make_identity

F32 = mybir.dt.float32
BF16 = mybir.dt.bfloat16
I32 = mybir.dt.int32
U32 = mybir.dt.uint32
U16 = mybir.dt.uint16
U8 = mybir.dt.uint8
FP8X4 = mybir.dt.float8_e4m3fn_x4
ALU = mybir.AluOpType
COPY = mybir.ActivationFunctionType.Copy

D, T, I, Q, E, Z, X = 512, 2048, 512, 128, 512, 1024, 1024
P = 128
FLOPS = 2 * Q * I * D + 2 * 2 * Q * I * E
HALF = I // 2
NB = E // P
W = 4 * P
LAST_SPLIT = 18


def tile_attend_passedthrough_twostores_lean_kernel(
    tc, query, keys_words, keys_scales, factor1, factor2, vals, vals2, offs, offs2, offs3, offs4, out
):
    nc = tc.nc
    with ExitStack() as ctx:
        sb = ctx.enter_context(tc.tile_pool(name="sb", bufs=1))
        ps = ctx.enter_context(tc.psum_pool(name="ps", bufs=1))

        def tile(shape, dtype, name, on=None):
            return sb.tile(shape, dtype, name=name, tag=on or name, align_bytes=64)

        def bank(shape, name, on=None):
            return ps.tile(shape, F32, name=name, tag=on or name)

        l1 = tile([P, I // 16], U16, "l1")
        l2 = tile([P, I // 16], U16, "l2")
        l3 = tile([P, I // 16], U16, "l3")
        l4 = tile([P, I // 16], U16, "l4")
        kw = tile([P, T], U32, "kw")
        ks = tile([P, T], U8, "ks")
        q_raw = tile([P, 4, Q], F32, "q_raw")
        f0 = tile([P, Z], F32, "f0")
        fac = [tile([P, 4], F32, "fac%d" % s) for s in range(2)]
        pool1 = [tile([P, T], F32, "pool1_%d" % j) for j in range(NB)]
        pool2 = [tile([P, X], F32, "pool2_%d" % j) for j in range(NB)]
        ident = tile([P, P], F32, "ident")

        nc.vector.memset(ks[:].bitcast(I32), 0)
        nc.vector.memset(f0[:], 0.0)
        make_identity(nc, ident[:])
        for s, factor in enumerate((factor1, factor2)):
            nc.gpsimd.dma_start(fac[s][:], factor.rearrange("o (p t) -> (o p) t", t=4))

        def load1(j):
            nc.sync.dma_start(pool1[j][:], vals[j * P : (j + 1) * P, :])

        def load2(j):
            nc.sync.dma_start(pool2[j][:], vals2[j * P : (j + 1) * P, :])

        nc.sync.dma_start(q_raw[:], query.rearrange("(p j) w -> p j w", j=4))
        nc.sync.dma_start(l1[:], offs)
        nc.sync.dma_start(kw[:].bitcast(I32), keys_words[0].rearrange("p n t -> p (n t)").bitcast(I32))
        scale_rows = keys_scales[0].rearrange("(g r) c -> r g c", r=4)
        for r in range(4):
            nc.sync.dma_start(ks[r:P:32, :].bitcast(I32), scale_rows[r].bitcast(I32))
        nc.sync.dma_start(l4[:], offs4)
        load2(0)
        load2(1)
        nc.sync.dma_start(l2[:], offs2)
        load2(2)
        nc.sync.dma_start(l3[:], offs3)
        load2(3)
        for j in range(NB):
            load1(j)

        def gather(engine, dst, window, lst):
            if engine == "V":
                nc.vector.tensor_copy(dst, window.indirect(lst))
            else:
                nc.scalar.activation(dst, window.indirect(lst), COPY)

        def turn(s, j, engine, turned):
            window, lst = (pool1[j], l1) if s == 0 else (pool2[j], l4)
            g = tile([P, I], BF16, "g%d_%d" % (s, j))
            if engine == "both":
                n = LAST_SPLIT * 16
                gather("V", g[:, :n], window[:], lst[:, :LAST_SPLIT])
                gather("S", g[:, n:], window[:], lst[:, LAST_SPLIT:])
            else:
                gather(engine, g[:], window[:], lst[:])
            words = g[:].bitcast(F32)
            for u in range(2):
                nc.tensor.transpose(turned[:, u, :], words[:, u::2], ident[:])

        def weave(engine, dst_words, turned):
            dst = dst_words.rearrange("p (b e u) -> p b e u", u=2, e=P)
            src = turned.rearrange("p b u e -> p b e u")
            if engine == "V":
                nc.vector.tensor_copy(dst, src)
            else:
                nc.scalar.copy(dst, src)

        def quantise(src, name, on=None):
            n = src.shape[1] // 4
            c = tile([P, n], U32, name + "_codes", on)
            sc = tile([P, n], U8, name + "_scales")
            nc.vector.quantize_mx(out=c[:].bitcast(FP8X4), scales=sc[:], in_=src)
            return c, sc

        def product(dst, lhs, lcols, rhs, rcols, start, stop):
            nc.tensor.matmul_mx(
                out=dst, lhsT=lhs[0][:, lcols].bitcast(FP8X4), lhsT_scale=lhs[1][:, lcols],
                rhs=rhs[0][:, rcols].bitcast(FP8X4), rhs_scale=rhs[1][:, rcols], start=start, stop=stop,
            )

        q_bf = tile([P, Q, 4], BF16, "q_bf")
        nc.scalar.activation(q_bf[:], q_raw[:].rearrange("p j w -> p w j"), COPY)

        q_mx = quantise(q_bf[:].rearrange("p w j -> p (w j)"), "q")

        t_ab = bank([P, 2, 2, P], "t_ab")
        t_cd = bank([P, 2, 2, P], "t_cd")
        turn(1, 0, "S", t_ab[:, 0])

        halves = [slice(h * 16, (h + 1) * 16) for h in range(2)]
        kg = [tile([P, HALF], U32, "kg%d" % h) for h in range(2)]
        for h in range(2):
            nc.vector.tensor_copy(kg[h][:], kw[:].indirect(l1[:, halves[h]]))
        a_sb = tile([P, I], F32, "a_sb", on="pool2_0")
        for h in range(2):
            sg = tile([P, HALF], U8, "sg%d" % h)
            nc.vector.tensor_copy(sg[:], ks[:].indirect(l1[:, halves[h]]))
            a_ps = bank([P, HALF], "a_ps%d" % h)
            product(a_ps[:], q_mx, slice(0, Q), (kg[h], sg), slice(0, HALF), True, True)
            slots = slice(h * HALF, (h + 1) * HALF)
            nc.scalar.copy(a_sb[:, slots], a_ps[:])
            nc.scalar.activation(f0[:].indirect(l2[:, halves[h]]), a_sb[:, slots], COPY)

        s_ps = bank([P, 4, Q], "s_ps")
        for t in range(4):
            nc.tensor.matmul(s_ps[:, t, :], a_sb[:, t::4], ident[:], start=(t == 0), stop=False, is_transpose=True)

        for j in range(1, NB):
            turn(1, j, "V", (t_ab, t_cd)[j // 2][:, j % 2])
        ab_bf = tile([P, 2 * W], BF16, "ab_bf", on="pool2_2")
        weave("V", ab_bf[:].bitcast(F32), t_ab[:])

        looked = tile([P, I], F32, "looked", on="pool2_3")
        nc.vector.tensor_copy(looked[:], f0[:].indirect(l3[:]))
        for t in range(4):
            nc.tensor.matmul(s_ps[:, t, :], looked[:, t::4], ident[:], start=False, stop=(t == 3), is_transpose=True)
        ab_mx = quantise(ab_bf[:], "ab", on="f0")


        t_ef = bank([P, 2, 2, P], "t_ef")
        turn(0, 0, "S", t_ef[:, 0])
        cd_bf = tile([P, 2 * W], BF16, "cd_bf", on="pool1_0")
        weave("S", cd_bf[:].bitcast(F32), t_cd[:])

        w_bf = tile([P, 2, Q, 4], BF16, "w_bf")
        for s in range(2):
            nc.vector.scalar_tensor_tensor(
                w_bf[:, s], s_ps[:].rearrange("p t q -> p q t"), 0.0,
                fac[s][:].unsqueeze(1).to_broadcast([P, Q, 4]), ALU.max, ALU.mult,
            )
        turn(0, 1, "S", t_ef[:, 1])
        w_mx = quantise(w_bf[:].rearrange("p s q t -> p (s q t)"), "w")
        w1, w2 = slice(0, Q), slice(Q, 2 * Q)
        cd_mx = quantise(cd_bf[:], "cd")

        t_g = bank([P, 1, 2, P], "t_g", on="t_ab")
        turn(0, 2, "S", t_g[:, 0])

        ef_bf = tile([P, 2 * W], BF16, "ef_bf")
        weave("V", ef_bf[:].bitcast(F32), t_ef[:])
        o01 = bank([P, 2 * P], "o01", on="t_ef")
        product(o01[:], w_mx, w2, ab_mx, slice(0, 2 * P), True, False)
        ef_mx = quantise(ef_bf[:], "ef")
        product(o01[:], w_mx, w1, ef_mx, slice(0, 2 * P), False, True)

        t_h = bank([P, 1, 2, P], "t_h", on="t_cd")
        turn(0, 3, "both", t_h[:, 0])

        late = tile([P, 7 * P], F32, "late", on="pool1_3")
        g_words, h_words, res = late[:, : 2 * P], late[:, 2 * P : 4 * P], late[:, 4 * P :]
        weave("V", g_words, t_g[:])
        nc.scalar.copy(res[:, : 2 * P], o01[:])
        nc.sync.dma_start(out[:, : 2 * P], res[:, : 2 * P])
        o2 = bank([P, P], "o2", on="t_ef")
        product(o2[:], w_mx, w2, cd_mx, slice(0, P), True, False)
        g_mx = quantise(g_words.bitcast(BF16), "g")
        product(o2[:], w_mx, w1, g_mx, slice(0, P), False, True)
        weave("S", h_words, t_h[:])
        o3 = bank([P, P], "o3", on="t_cd")
        product(o3[:], w_mx, w2, cd_mx, slice(P, 2 * P), True, False)
        h_mx = quantise(h_words.bitcast(BF16), "h")
        product(o3[:], w_mx, w1, h_mx, slice(0, P), False, True)
        nc.scalar.copy(res[:, 2 * P :], o2[:])
        nc.sync.dma_start(out[:, 2 * P : 3 * P], res[:, 2 * P :])
        res3 = tile([P, P], F32, "res3")
        nc.vector.tensor_copy(res3[:], o3[:])
        nc.sync.dma_start(out[:, 3 * P :], res3[:])
